import numpy as np
import ml_dtypes


def mxq(x, axis, fmt="e4m3"):
    dtype, down = {"e4m3": (ml_dtypes.float8_e4m3fn, 7), "e5m2": (ml_dtypes.float8_e5m2, 14)}[fmt]
    v = np.moveaxis(np.asarray(x, np.float32).astype(ml_dtypes.bfloat16).astype(np.float64), axis, -1)
    blocks = v.reshape(v.shape[:-1] + (-1, 32))
    amax = np.abs(blocks).max(-1, keepdims=True)
    byte = np.maximum(np.where(amax > 0, np.frexp(amax)[1] - 1 + 127, 0) - down, 1)
    scale = np.exp2(byte - 127.0)
    codes = (blocks / scale).astype(np.float32).astype(dtype).astype(np.float64)
    return np.moveaxis((codes * scale).reshape(v.shape), -1, axis)


WIDE = False


def mx_kscale(k):
    if not WIDE:
        return np.ones(k)
    levels = np.array([10, -10, 5, -5, 0])
    if k % 512:
        return np.exp2(np.random.permutation(np.resize(levels, k // 32))).repeat(32)
    a = np.empty((k // 512, 16))
    for p in range(k // 512):
        a[p, :8] = np.random.permutation(np.resize(levels, 8))
        for g in range(8):
            far = levels[np.abs(levels - a[p, g]) >= 10]
            a[p, g + 8] = far[np.random.randint(len(far))]
    return np.exp2(a.ravel()).repeat(32)


BF16 = ml_dtypes.bfloat16


def bf(x):
    return np.asarray(x, np.float32).astype(BF16)


def f64(x):
    return np.asarray(x).astype(np.float64)


E2M1 = np.array([0.0, 0.5, 1.0, 1.5, 2.0, 3.0, 4.0, 6.0, -0.0, -0.5, -1.0, -1.5, -2.0, -3.0, -4.0, -6.0])


def pack_weight(w, fmt):
    k, n = w.shape
    w = f64(bf(w)).reshape(k // 32, 32, n)
    amax = np.abs(w).max(1)
    if fmt == "e4m3":
        byte = np.frexp(amax)[1] - 1 + 127 - 7
    else:
        mant, ex = np.frexp(amax / 6.0)
        byte = np.where(mant > 0.5, ex, ex - 1) + 127
    byte = np.clip(np.where(amax > 0, byte, 1), 1, 254)
    scaled = (w * np.exp2(127.0 - byte)[:, None, :]).reshape(k, n).astype(np.float32)
    by_word = np.ascontiguousarray(scaled.reshape(k // 512, 128, 4, n).transpose(0, 1, 3, 2))
    if fmt == "e4m3":
        words = by_word.astype(ml_dtypes.float8_e4m3fn).view(np.uint8)
    else:
        c = by_word.astype(ml_dtypes.float4_e2m1fn).view(np.uint8) & 0xF
        words = c[..., 0::2] | (c[..., 1::2] << 4)
    return np.ascontiguousarray(words), np.ascontiguousarray(byte.astype(np.uint8).reshape(k // 512, 16, n))


def unpack_weight(words, scales, fmt):
    g, p, n, _ = words.shape
    if fmt == "e4m3":
        vals = np.ascontiguousarray(words).view(ml_dtypes.float8_e4m3fn).astype(np.float64)
    else:
        nib = np.empty((g, p, n, 4), np.uint8)
        nib[..., 0::2] = words & 0xF
        nib[..., 1::2] = words >> 4
        vals = E2M1[nib]
    vals = vals * np.repeat(np.exp2(scales.astype(np.float64) - 127.0), 8, axis=1)[..., None]
    return vals.transpose(0, 1, 3, 2).reshape(g * 512, n)
def pack4(w):
    words, scales = pack_weight(w, "e2m1")
    return words.reshape(words.shape[0], 128, -1), scales


def unpack4(words, scales):
    return unpack_weight(words.reshape(words.shape[0], 128, -1, 2), scales, "e2m1")


M, U, H, F = 512, 1536, 1024, 2048

STAY = 0.5
SPREAD = 0.5


def setup_inputs():
    s, r, t = mx_kscale(U), mx_kscale(H), mx_kscale(U)
    step = STAY * np.eye(U) + SPREAD * np.random.standard_normal((U, U)) / np.sqrt(U)
    known = SPREAD * np.random.standard_normal((H, U)) / np.sqrt(H)
    up = np.random.standard_normal((U, F)) / np.sqrt(U)
    known_words, known_scales = pack4(known / r[:, None] * t)
    up_words, up_scales = pack4(up / t[:, None])
    return {"alpha": bf(np.random.random_sample((M, U)) * s),
            "fixed": bf(np.random.random_sample((M, H)) * r),
            "step": bf(step / s[:, None] * t),
            "known_words": known_words, "known_scales": known_scales,
            "pull": bf(0.5 * np.random.random_sample((M, U)) * t),
            "cap": bf((1 - 0.2 * np.random.random_sample(U)) * t),
            "up_words": up_words, "up_scales": up_scales}


def reference(alpha, fixed, step, known_words, known_scales, pull, cap, up_words, up_scales):
    known = unpack4(known_words, known_scales)
    up = unpack4(up_words, up_scales)
    z = (mxq(f64(alpha), 1, "e4m3") @ mxq(f64(step), 0, "e4m3")) + (mxq(f64(fixed), 1, "e4m3") @ known)
    new = np.minimum(np.maximum(z + f64(pull), 0.0), f64(cap))
    return mxq(new, 1, "e4m3") @ up

@@ -1,0 +1,397 @@
+from contextlib import ExitStack
+
+import concourse.mybir as mybir
+from concourse.masks import make_identity
+
+M, U, H, F = 512, 1536, 1024, 2048
+FLOPS = 2 * M * (U * U + H * U + U * F)
+
+F32 = mybir.dt.float32
+BF16 = mybir.dt.bfloat16
+I32 = mybir.dt.int32
+U32 = mybir.dt.uint32
+U8 = mybir.dt.uint8
+FP8X4 = mybir.dt.float8_e4m3fn_x4
+FP4X4 = mybir.dt.float4_e2m1fn_x4
+ALU = mybir.AluOpType
+
+P = 128
+PACK = 4
+KP = P * PACK
+N = 512
+MT = M // P
+HG = H // KP
+UG = U // KP
+FT = F // N
+
+
+def tile_matting_clipped_step_s3_kernel(
+    tc, alpha, fixed, step, known_words, known_scales, pull, cap, up_words, up_scales, out
+):
+    nc = tc.nc
+    with ExitStack() as ctx:
+        keep = ctx.enter_context(tc.tile_pool(name="keep", bufs=1))
+        flow = ctx.enter_context(tc.tile_pool(name="flow", bufs=4))
+        psum = ctx.enter_context(tc.psum_pool(name="psum", bufs=1))
+        ctx.enter_context(tc.manual_schedule())
+
+        def kept(name, shape, dtype):
+            return keep.tile(shape, dtype, name=name, align_bytes=64)
+
+        def bank(b, name):
+            return psum.tile([P, N], F32, name=name, tag="bank%d" % b)
+
+        ident = kept("ident", [P, P], F32)
+        make_identity(nc, ident[:])
+        known_plane = kept("known_plane", [P, HG, U], U8)
+        up_plane = [kept("up_plane%d" % h, [P, UG, F // 2], U8) for h in range(2)]
+        nc.vector.memset(known_plane[:].bitcast(I32), 0)
+
+        for h in range(2):
+            nc.vector.memset(up_plane[h][:].bitcast(I32), 0)
+
+        act_raw = {}
+
+        def load_act(j, h0, h1):
+            src = fixed[:, j * KP:(j + 1) * KP] if j < HG else alpha[:, (j - HG) * KP:(j - HG + 1) * KP]
+            t = kept("act_raw%d_%d" % (j, h0), [P, 2 * (h1 - h0), KP], BF16)
+            nc.sync.dma_start(out=t[:], in_=src.rearrange("(m p) k -> p m k", p=P)[:, 2 * h0:2 * h1, :])
+            for h in range(h0, h1):
+                act_raw[(j, h)] = t[:, 2 * (h - h0):2 * (h - h0) + 2, :]
+
+        def load_scales(plane, scales):
+            for q in range(4):
+                nc.sync.dma_start(
+                    out=plane[32 * q:32 * q + 4].bitcast(I32),
+                    in_=scales[:, 4 * q:4 * q + 4, :].rearrange("g r n -> r g n").bitcast(I32),
+                )
+
+        known_sb = {}
+
+        def load_known(g0, g1, c0, c1):
+            t = kept("known%d_%d" % (g0, c0), [P, g1 - g0, 2 * N * (c1 - c0)], U8)
+            nc.sync.dma_start(
+                out=t[:].bitcast(I32),
+                in_=known_words[g0:g1, :, 2 * N * c0:2 * N * c1].rearrange("g p n -> p g n").bitcast(I32),
+            )
+            for g in range(g0, g1):
+                for c in range(c0, c1):
+                    known_sb[(g, c)] = t[:, g - g0, 2 * N * (c - c0):2 * N * (c - c0 + 1)]
+
+        step_raw = {}
+
+        def load_step(c, g):
+            step_raw[(c, g)] = kept("step_raw%d_%d" % (c, g), [P, PACK, N], BF16)
+            rows = step[g * KP:(g + 1) * KP, c * N:(c + 1) * N]
+            nc.sync.dma_start(out=step_raw[(c, g)][:], in_=rows.rearrange("(p t) n -> p t n", t=PACK))
+
+        pull_sb = {}
+
+        def load_pull(c):
+            pull_sb[c] = kept("pull%d" % c, [P, MT, N], BF16)
+            nc.sync.dma_start(out=pull_sb[c][:], in_=pull[:, c * N:(c + 1) * N].rearrange("(m p) n -> p m n", p=P))
+
+        up_sb = {}
+
+        def load_up(h):
+            load_scales(up_plane[h], up_scales[:, :, h * (F // 2):(h + 1) * (F // 2)])
+            up_sb[h] = kept("up%d" % h, [P, UG, F], U8)
+            nc.sync.dma_start(
+                out=up_sb[h][:].bitcast(I32),
+                in_=up_words[:, :, h * F:(h + 1) * F].rearrange("g p n -> p g n").bitcast(I32),
+            )
+
+        cap_sb = kept("cap_sb", [P, UG, PACK], BF16)
+        nc.scalar.dma_start(out=cap_sb[:], in_=cap.rearrange("(g p t) -> p g t", p=P, t=PACK))
+
+
+        load_act(0, 0, 1)
+        load_act(0, 1, 2)
+        load_scales(known_plane, known_scales)
+        load_known(0, 1, 0, 2)
+        load_act(1, 0, 2)
+        load_known(1, 2, 0, 2)
+        load_step(0, 0)
+        load_act(2, 0, 2)
+        load_step(0, 1)
+        load_act(3, 0, 2)
+        load_step(0, 2)
+        load_act(4, 0, 2)
+        load_step(1, 0)
+        load_step(1, 1)
+        load_pull(0)
+        load_step(1, 2)
+        load_known(0, 2, 2, 3)
+        load_step(2, 0)
+        load_step(2, 1)
+        load_step(2, 2)
+        load_pull(1)
+        load_up(0)
+        load_pull(2)
+        load_up(1)
+
+
+        cap_wide = kept("cap_wide", [P, UG, P, PACK], BF16)
+        nc.vector.tensor_copy(out=cap_wide[:], in_=cap_sb[:].unsqueeze(2).to_broadcast([P, UG, P, PACK]))
+
+        def words_out(engine, dst, src_bank, n_ops):
+            d = dst.bitcast(F32).rearrange("p (o r u) -> p o r u", o=n_ops, u=2)
+            s = src_bank[:, :n_ops * 2 * P].rearrange("p (o u r) -> p o r u", o=n_ops, u=2)
+            if engine == "S":
+                nc.scalar.copy(out=d, in_=s)
+            else:
+                nc.vector.tensor_copy(out=d, in_=s)
+
+        act_t, act_codes, act_scales, act_bank = {}, {}, {}, {}
+
+        def turn_act(j, h, b):
+            act_bank[(j, h)] = bank(b, "act_bank%d_%d" % (j, h))
+            for o in range(2):
+                words = act_raw[(j, h)][:, o, :].bitcast(F32)
+                for u in range(2):
+                    s = 2 * o + u
+                    nc.tensor.transpose(act_bank[(j, h)][:, s * P:(s + 1) * P], words[:, u::2], ident[:])
+
+        def out_act(j, h, engine):
+            if h == 0:
+                act_t[j] = flow.tile([P, MT * KP], BF16, name="act_t%d" % j, tag="grouped", align_bytes=64)
+            words_out(engine, act_t[j][:, 2 * h * KP:2 * (h + 1) * KP], act_bank[(j, h)], 2)
+
+        def quant_act(j, h0=0, h1=2):
+            if h0 == 0:
+                act_codes[j] = kept("act_codes%d" % j, [P, M], U32)
+                act_scales[j] = kept("act_scales%d" % j, [P, M], U8)
+            cols = slice(2 * h0 * P, 2 * h1 * P)
+            nc.vector.quantize_mx(
+                out=act_codes[j][:, cols].bitcast(FP8X4),
+                scales=act_scales[j][:, cols],
+                in_=act_t[j][:, 2 * h0 * KP:2 * h1 * KP],
+            )
+
+        step_t, step_codes, step_scales = {}, {}, {}
+
+        def weave(c, g, v_cols):
+            step_t[(c, g)] = flow.tile([P, N * PACK], BF16, name="step_t%d_%d" % (c, g), tag="grouped", align_bytes=64)
+            d = step_t[(c, g)][:].rearrange("p (a i t) -> p a t i", i=4, t=PACK)
+            s = step_raw[(c, g)][:].rearrange("p t (a i) -> p a t i", i=4)
+            nc.scalar.copy(out=d[:, v_cols // 4:], in_=s[:, v_cols // 4:])
+            nc.vector.tensor_copy(out=d[:, :v_cols // 4], in_=s[:, :v_cols // 4])
+
+        def quant_step(c, g):
+            step_codes[(c, g)] = kept("step_codes%d_%d" % (c, g), [P, N], U32)
+            step_scales[(c, g)] = kept("step_scales%d_%d" % (c, g), [P, N], U8)
+            nc.vector.quantize_mx(
+                out=step_codes[(c, g)][:].bitcast(FP8X4), scales=step_scales[(c, g)][:], in_=step_t[(c, g)][:]
+            )
+
+        z_bank = {}
+
+        def z_pass(j, c, ms, first_bank=None):
+            for m in ms:
+                if j == 0:
+                    z_bank[(c, m)] = bank(first_bank + m, "z%d_%d" % (c, m))
+                if j < HG:
+                    rhs = known_sb[(j, c)].bitcast(FP4X4)
+                    rhs_scale = known_plane[:, j, c * N:(c + 1) * N]
+                else:
+                    rhs = step_codes[(c, j - HG)][:].bitcast(FP8X4)
+                    rhs_scale = step_scales[(c, j - HG)][:]
+                nc.tensor.matmul_mx(
+                    out=z_bank[(c, m)][:],
+                    lhsT=act_codes[j][:, m * P:(m + 1) * P].bitcast(FP8X4),
+                    lhsT_scale=act_scales[j][:, m * P:(m + 1) * P],
+                    rhs=rhs,
+                    rhs_scale=rhs_scale,
+                    start=(j == 0),
+                    stop=(j == HG + UG - 1),
+                )
+
+        summed = {}
+
+        def add_pull(c, m):
+            summed[(c, m)] = kept("summed%d_%d" % (c, m), [P, N], BF16)
+            nc.vector.tensor_tensor(
+                out=summed[(c, m)][:].rearrange("r (u p e) -> r u p e", u=2, e=2),
+                in0=z_bank[(c, m)][:].rearrange("r (p u e) -> r u p e", u=2, e=2),
+                in1=pull_sb[c][:, m, :].rearrange("r (p u e) -> r u p e", u=2, e=2),
+                op=ALU.add,
+            )
+
+        new_bank, new_t, new_clip, new_codes, new_scales = {}, {}, {}, {}, {}
+
+        def turn_new(ops, b):
+            new_bank[ops] = bank(b, "new_bank%d_%d" % ops[0])
+            for o, cm in enumerate(ops):
+                words = summed[cm][:].bitcast(F32)
+                for u in range(2):
+                    s = 2 * o + u
+                    nc.tensor.transpose(new_bank[ops][:, s * P:(s + 1) * P], words[:, u * P:(u + 1) * P], ident[:])
+
+        def out_new(ops, engine):
+            new_t[ops] = kept("new_t%d_%d" % ops[0], [P, len(ops) * KP], BF16)
+            words_out(engine, new_t[ops][:], new_bank[ops], len(ops))
+
+        def clip_new(ops):
+            new_clip[ops] = kept("new_clip%d_%d" % ops[0], [P, len(ops) * KP], BF16)
+            caps = cap_wide[:].rearrange("p g r t -> p g (r t)")
+            c0 = ops[0][0]
+            if ops[-1][0] == c0:
+                caps = caps[:, c0:c0 + 1, :].to_broadcast([P, len(ops), KP])
+            else:
+                caps = caps[:, c0:c0 + len(ops), :]
+            nc.vector.scalar_tensor_tensor(
+                out=new_clip[ops][:].rearrange("p (o k) -> p o k", k=KP),
+                in0=new_t[ops][:].rearrange("p (o k) -> p o k", k=KP),
+                scalar=0.0,
+                in1=caps,
+                op0=ALU.max,
+                op1=ALU.min,
+            )
+
+        def quant_new(ops):
+            codes = kept("new_codes%d_%d" % ops[0], [P, len(ops) * P], U32)
+            scales = kept("new_scales%d_%d" % ops[0], [P, len(ops) * P], U8)
+            nc.vector.quantize_mx(out=codes[:].bitcast(FP8X4), scales=scales[:], in_=new_clip[ops][:])
+            for o, cm in enumerate(ops):
+                new_codes[cm] = codes[:, o * P:(o + 1) * P]
+                new_scales[cm] = scales[:, o * P:(o + 1) * P]
+
+        out_bank = {}
+
+        def up_pass(m, f, gs, b=None):
+            h, fh = divmod(f, 2)
+            for g in gs:
+                if g == 0:
+                    out_bank[(m, f)] = bank(b, "out%d_%d" % (m, f))
+                nc.tensor.matmul_mx(
+                    out=out_bank[(m, f)][:],
+                    lhsT=new_codes[(g, m)].bitcast(FP8X4),
+                    lhsT_scale=new_scales[(g, m)],
+                    rhs=up_sb[h][:, g, 2 * fh * N:2 * (fh + 1) * N].bitcast(FP4X4),
+                    rhs_scale=up_plane[h][:, g, fh * N:(fh + 1) * N],
+                    start=(g == 0),
+                    stop=(g == UG - 1),
+                )
+
+        def store(m, f, engine):
+            res = flow.tile([P, N], F32, name="res%d_%d" % (m, f), tag="res", bufs=8)
+            if engine == "S":
+                nc.scalar.copy(out=res[:], in_=out_bank[(m, f)][:])
+            else:
+                nc.vector.tensor_copy(out=res[:], in_=out_bank[(m, f)][:])
+            nc.sync.dma_start(out=out[m * P:(m + 1) * P, f * N:(f + 1) * N], in_=res[:])
+
+
+        ALL = range(MT)
+
+        def act(j, e1):
+            turn_act(j, 0, 6)
+            turn_act(j, 1, 7)
+            out_act(j, 0, "S")
+            out_act(j, 1, e1)
+
+        act(0, "S")
+        quant_act(0, 0, 1)
+        quant_act(0, 1, 2)
+        z_pass(0, 0, [0, 1], 0)
+        z_pass(0, 1, [0], 4)
+        act(1, "V")
+        z_pass(0, 1, [1], 4)
+        z_pass(0, 0, [2, 3], 0)
+        weave(0, 0, 256)
+        quant_act(1)
+        act(2, "S")
+        quant_step(0, 0)
+        z_pass(1, 0, ALL)
+        z_pass(1, 1, [0, 1])
+        weave(0, 1, 352)
+        quant_act(2)
+        act(3, "S")
+        quant_step(0, 1)
+        z_pass(2, 0, ALL)
+        weave(0, 2, 352)
+        quant_act(3)
+        act(4, "S")
+        quant_step(0, 2)
+        z_pass(3, 0, ALL)
+        weave(1, 0, 352)
+        quant_act(4)
+        z_pass(0, 1, [2, 3], 4)
+        z_pass(1, 1, [2, 3])
+        quant_step(1, 0)
+        z_pass(4, 0, ALL)
+        weave(1, 1, 256)
+        z_pass(2, 1, ALL)
+        weave(1, 2, 192)
+        quant_step(1, 1)
+        add_pull(0, 0)
+        z_pass(3, 1, ALL)
+        quant_step(1, 2)
+        add_pull(0, 1)
+        z_pass(4, 1, ALL)
+        weave(2, 0, 128)
+        add_pull(0, 2)
+        add_pull(0, 3)
+        z_pass(0, 2, ALL, 0)
+        z_pass(1, 2, ALL)
+        quant_step(2, 0)
+        weave(2, 1, 128)
+        add_pull(1, 0)
+        quant_step(2, 1)
+        weave(2, 2, 128)
+        add_pull(1, 1)
+        z_pass(2, 2, ALL)
+        low = [((0, m), (1, m)) for m in ALL]
+        last = [((2, 0), (2, 1)), ((2, 2), (2, 3))]
+        turn_new(low[0], 4)
+        turn_new(low[1], 5)
+        out_new(low[0], "S")
+        out_new(low[1], "S")
+        add_pull(1, 2)
+        quant_step(2, 2)
+        add_pull(1, 3)
+        z_pass(3, 2, ALL)
+        turn_new(low[2], 6)
+        turn_new(low[3], 7)
+        out_new(low[2], "S")
+        out_new(low[3], "S")
+        clip_new(low[0])
+        clip_new(low[1])
+        quant_new(low[0])
+        z_pass(4, 2, ALL)
+        quant_new(low[1])
+        add_pull(2, 0)
+        add_pull(2, 1)
+        up_pass(0, 0, [0, 1], 4)
+        up_pass(0, 1, [0, 1], 5)
+        turn_new(last[0], 0)
+        out_new(last[0], "S")
+        add_pull(2, 2)
+        add_pull(2, 3)
+        up_pass(1, 0, [0, 1], 6)
+        up_pass(1, 1, [0, 1], 7)
+        turn_new(last[1], 1)
+        out_new(last[1], "S")
+        clip_new(low[2])
+        clip_new(last[0])
+        quant_new(low[2])
+        quant_new(last[0])
+        clip_new(low[3])
+        clip_new(last[1])
+        quant_new(low[3])
+        quant_new(last[1])
+        up_pass(2, 0, [0, 1], 2)
+        up_pass(2, 1, [0, 1], 3)
+        for m, f in [(0, 0), (0, 1), (1, 0), (1, 1)]:
+            up_pass(m, f, [2])
+            store(m, f, "S")
+        up_pass(3, 0, [0, 1], 0)
+        up_pass(3, 1, [0, 1], 1)
+        for i, (m, f) in enumerate([(2, 0), (2, 1), (3, 0), (3, 1)]):
+            up_pass(m, f, [2])
+            store(m, f, "V" if i % 2 == 0 else "S")
+        rest = [(m, f) for m in ALL for f in (2, 3)]
+        banks = [4, 5, 6, 7, 2, 3, 0, 1]
+        for i, (m, f) in enumerate(rest):
+            up_pass(m, f, range(UG), banks[i % 8])
+            store(m, f, "V" if i % 2 == 0 else "S")

@@ -102,7 +102,9 @@ def tile_matting_clipped_step_s3_kernel(
             )
 
         cap_sb = kept("cap_sb", [P, UG, PACK], BF16)
-        nc.scalar.dma_start(out=cap_sb[:], in_=cap.rearrange("(g p t) -> p g t", p=P, t=PACK))
+
+        def load_cap():
+            nc.sync.dma_start(out=cap_sb[:], in_=cap.rearrange("(g p t) -> p g t", p=P, t=PACK))
 
 
         load_act(0, 0, 1)
@@ -120,6 +122,7 @@ def tile_matting_clipped_step_s3_kernel(
         load_step(1, 0)
         load_step(1, 1)
         load_pull(0)
+        load_cap()
         load_step(1, 2)
         load_known(0, 2, 2, 3)
         load_step(2, 0)
@@ -130,9 +133,6 @@ def tile_matting_clipped_step_s3_kernel(
         load_pull(2)
         load_up(1)
 
-
-        cap_wide = kept("cap_wide", [P, UG, P, PACK], BF16)
-        nc.vector.tensor_copy(out=cap_wide[:], in_=cap_sb[:].unsqueeze(2).to_broadcast([P, UG, P, PACK]))
 
         def words_out(engine, dst, src_bank, n_ops):
             d = dst.bitcast(F32).rearrange("p (o r u) -> p o r u", o=n_ops, u=2)
@@ -175,7 +175,8 @@ def tile_matting_clipped_step_s3_kernel(
             d = step_t[(c, g)][:].rearrange("p (a i t) -> p a t i", i=4, t=PACK)
             s = step_raw[(c, g)][:].rearrange("p t (a i) -> p a t i", i=4)
             nc.scalar.copy(out=d[:, v_cols // 4:], in_=s[:, v_cols // 4:])
-            nc.vector.tensor_copy(out=d[:, :v_cols // 4], in_=s[:, :v_cols // 4])
+            if v_cols:
+                nc.vector.tensor_copy(out=d[:, :v_cols // 4], in_=s[:, :v_cols // 4])
 
         def quant_step(c, g):
             step_codes[(c, g)] = kept("step_codes%d_%d" % (c, g), [P, N], U32)
@@ -227,25 +228,26 @@ def tile_matting_clipped_step_s3_kernel(
                     s = 2 * o + u
                     nc.tensor.transpose(new_bank[ops][:, s * P:(s + 1) * P], words[:, u * P:(u + 1) * P], ident[:])
 
-        def out_new(ops, engine):
+        def out_new(ops):
             new_t[ops] = kept("new_t%d_%d" % ops[0], [P, len(ops) * KP], BF16)
-            words_out(engine, new_t[ops][:], new_bank[ops], len(ops))
+            pairs = new_bank[ops][:].bitcast(BF16)
+            for o in range(len(ops)):
+                nc.scalar.activation(
+                    out=new_t[ops][:, o * KP:(o + 1) * KP].rearrange("p (r u e) -> p r u e", u=2, e=2),
+                    in_=pairs[:, o * KP:(o + 1) * KP].rearrange("p (u r e) -> p r u e", u=2, e=2),
+                    func=mybir.ActivationFunctionType.Relu,
+                )
 
         def clip_new(ops):
             new_clip[ops] = kept("new_clip%d_%d" % ops[0], [P, len(ops) * KP], BF16)
-            caps = cap_wide[:].rearrange("p g r t -> p g (r t)")
             c0 = ops[0][0]
-            if ops[-1][0] == c0:
-                caps = caps[:, c0:c0 + 1, :].to_broadcast([P, len(ops), KP])
-            else:
-                caps = caps[:, c0:c0 + len(ops), :]
-            nc.vector.scalar_tensor_tensor(
-                out=new_clip[ops][:].rearrange("p (o k) -> p o k", k=KP),
-                in0=new_t[ops][:].rearrange("p (o k) -> p o k", k=KP),
-                scalar=0.0,
+            c1 = ops[-1][0] + 1
+            caps = cap_sb[:, c0:c1, :].unsqueeze(2).to_broadcast([P, len(ops), P, PACK])
+            nc.vector.tensor_tensor(
+                out=new_clip[ops][:].rearrange("p (o r t) -> p o r t", r=P, t=PACK),
+                in0=new_t[ops][:].rearrange("p (o r t) -> p o r t", r=P, t=PACK),
                 in1=caps,
-                op0=ALU.max,
-                op1=ALU.min,
+                op=ALU.min,
             )
 
         def quant_new(ops):
@@ -273,13 +275,33 @@ def tile_matting_clipped_step_s3_kernel(
                     stop=(g == UG - 1),
                 )
 
-        def store(m, f, engine):
-            res = flow.tile([P, N], F32, name="res%d_%d" % (m, f), tag="res", bufs=8)
+        def leave(src, m, col, width, engine):
+            res = flow.tile([P, width], F32, name="res%d_%d" % (m, col), tag="res", bufs=16)
             if engine == "S":
-                nc.scalar.copy(out=res[:], in_=out_bank[(m, f)][:])
+                nc.scalar.copy(out=res[:], in_=src)
             else:
-                nc.vector.tensor_copy(out=res[:], in_=out_bank[(m, f)][:])
-            nc.sync.dma_start(out=out[m * P:(m + 1) * P, f * N:(f + 1) * N], in_=res[:])
+                nc.vector.tensor_copy(out=res[:], in_=src)
+            nc.sync.dma_start(out=out[m * P:(m + 1) * P, col:col + width], in_=res[:])
+
+        def store(m, f, engine):
+            leave(out_bank[(m, f)][:], m, f * N, N, engine)
+
+        def narrow(m, f, banks):
+            h, fh = divmod(f, 2)
+            for i, b in enumerate(banks):
+                acc = bank(b, "tail%d" % i)
+                col = fh * N + i * P
+                for g in range(UG):
+                    nc.tensor.matmul_mx(
+                        out=acc[:, :P],
+                        lhsT=new_codes[(g, m)].bitcast(FP8X4),
+                        lhsT_scale=new_scales[(g, m)],
+                        rhs=up_sb[h][:, g, 2 * col:2 * (col + P)].bitcast(FP4X4),
+                        rhs_scale=up_plane[h][:, g, col:col + P],
+                        start=(g == 0),
+                        stop=(g == UG - 1),
+                    )
+                leave(acc[:, :P], m, f * N + i * P, P, "V" if i % 2 == 0 else "S")
 
 
         ALL = range(MT)
@@ -335,63 +357,68 @@ def tile_matting_clipped_step_s3_kernel(
         z_pass(0, 2, ALL, 0)
         z_pass(1, 2, ALL)
         quant_step(2, 0)
-        weave(2, 1, 128)
+        weave(2, 1, 64)
         add_pull(1, 0)
         quant_step(2, 1)
-        weave(2, 2, 128)
+        weave(2, 2, 64)
         add_pull(1, 1)
         z_pass(2, 2, ALL)
         low = [((0, m), (1, m)) for m in ALL]
-        last = [((2, 0), (2, 1)), ((2, 2), (2, 3))]
+        top = [((2, m),) for m in ALL]
+        pair = ((2, 2), (2, 3))
         turn_new(low[0], 4)
         turn_new(low[1], 5)
-        out_new(low[0], "S")
-        out_new(low[1], "S")
+        out_new(low[0])
+        out_new(low[1])
         add_pull(1, 2)
         quant_step(2, 2)
         add_pull(1, 3)
-        z_pass(3, 2, ALL)
+        z_pass(3, 2, [0, 1, 2])
+        z_pass(4, 2, [0])
+        z_pass(3, 2, [3])
+        z_pass(4, 2, [1, 2, 3])
+        add_pull(2, 0)
+        clip_new(low[0])
+        quant_new(low[0])
+        add_pull(2, 1)
         turn_new(low[2], 6)
         turn_new(low[3], 7)
-        out_new(low[2], "S")
-        out_new(low[3], "S")
-        clip_new(low[0])
-        clip_new(low[1])
-        quant_new(low[0])
-        z_pass(4, 2, ALL)
-        quant_new(low[1])
-        add_pull(2, 0)
-        add_pull(2, 1)
+        turn_new(top[0], 0)
+        out_new(top[0])
+        out_new(low[2])
         up_pass(0, 0, [0, 1], 4)
         up_pass(0, 1, [0, 1], 5)
-        turn_new(last[0], 0)
-        out_new(last[0], "S")
+        turn_new(top[1], 1)
+        out_new(top[1])
+        out_new(low[3])
+        clip_new(low[1])
+        clip_new(top[0])
+        quant_new(low[1])
+        quant_new(top[0])
+        up_pass(0, 2, [0, 1], 0)
+        up_pass(0, 0, [2])
+        up_pass(0, 1, [2])
+        up_pass(0, 2, [2])
         add_pull(2, 2)
+        clip_new(top[1])
         add_pull(2, 3)
-        up_pass(1, 0, [0, 1], 6)
-        up_pass(1, 1, [0, 1], 7)
-        turn_new(last[1], 1)
-        out_new(last[1], "S")
+        quant_new(top[1])
+        store(0, 0, "S")
+        store(0, 1, "S")
+        up_pass(0, 3, range(UG), 1)
+        turn_new(pair, 2)
+        out_new(pair)
         clip_new(low[2])
-        clip_new(last[0])
+        store(0, 2, "V")
         quant_new(low[2])
-        quant_new(last[0])
+        store(0, 3, "S")
+        clip_new(pair)
         clip_new(low[3])
-        clip_new(last[1])
+        quant_new(pair)
         quant_new(low[3])
-        quant_new(last[1])
-        up_pass(2, 0, [0, 1], 2)
-        up_pass(2, 1, [0, 1], 3)
-        for m, f in [(0, 0), (0, 1), (1, 0), (1, 1)]:
-            up_pass(m, f, [2])
-            store(m, f, "S")
-        up_pass(3, 0, [0, 1], 0)
-        up_pass(3, 1, [0, 1], 1)
-        for i, (m, f) in enumerate([(2, 0), (2, 1), (3, 0), (3, 1)]):
-            up_pass(m, f, [2])
-            store(m, f, "V" if i % 2 == 0 else "S")
-        rest = [(m, f) for m in ALL for f in (2, 3)]
-        banks = [4, 5, 6, 7, 2, 3, 0, 1]
-        for i, (m, f) in enumerate(rest):
+        rest = [(m, f) for m in (1, 2, 3) for f in range(FT)]
+        banks = [3, 4, 5, 6, 0, 1, 7, 2]
+        for i, (m, f) in enumerate(rest[:-1]):
             up_pass(m, f, range(UG), banks[i % 8])
-            store(m, f, "V" if i % 2 == 0 else "S")
+            store(m, f, "S" if i % 2 == 0 else "V")
+        narrow(3, 3, [6, 0, 1, 7])

@@ -43,10 +43,29 @@ def tile_matting_clipped_step_s3_kernel(
 
         ident = kept("ident", [P, P], F32)
         make_identity(nc, ident[:])
-        known_plane = kept("known_plane", [P, HG, U], U8)
+        known_plane = [kept("known_plane0", [P, HG, 2 * N], U8), kept("known_plane1", [P, HG, N], U8)]
         up_plane = [kept("up_plane%d" % h, [P, UG, F // 2], U8) for h in range(2)]
-        nc.vector.memset(known_plane[:].bitcast(I32), 0)
+        nc.vector.memset(known_plane[0][:].bitcast(I32), 0)
+        warm_in = kept("warm_in", [P, 2 * KP], BF16)
+        warm_codes = kept("warm_codes", [P, 2 * P], U32)
+        warm_scales = kept("warm_scales", [P, 2 * P], U8)
+        nc.vector.memset(warm_in[:], 0.0)
+        nc.vector.quantize_mx(out=warm_codes[:].bitcast(FP8X4), scales=warm_scales[:], in_=warm_in[:])
 
+        def warm(n, b):
+            sink = bank(b, "warm%d" % b)
+            for i in range(n):
+                nc.tensor.matmul_mx(
+                    out=sink[:, :2 * P],
+                    lhsT=warm_codes[:, :P].bitcast(FP8X4),
+                    lhsT_scale=warm_scales[:, :P],
+                    rhs=warm_codes[:].bitcast(FP8X4),
+                    rhs_scale=warm_scales[:],
+                    start=True,
+                    stop=True,
+                )
+
+        nc.vector.memset(known_plane[1][:].bitcast(I32), 0)
         for h in range(2):
             nc.vector.memset(up_plane[h][:].bitcast(I32), 0)
 
@@ -87,9 +106,12 @@ def tile_matting_clipped_step_s3_kernel(
 
         pull_sb = {}
 
-        def load_pull(c):
-            pull_sb[c] = kept("pull%d" % c, [P, MT, N], BF16)
-            nc.sync.dma_start(out=pull_sb[c][:], in_=pull[:, c * N:(c + 1) * N].rearrange("(m p) n -> p m n", p=P))
+        def load_pull(c, m0=0, m1=MT):
+            t = kept("pull%d_%d" % (c, m0), [P, m1 - m0, N], BF16)
+            rows = pull[m0 * P:m1 * P, c * N:(c + 1) * N]
+            nc.sync.dma_start(out=t[:], in_=rows.rearrange("(m p) n -> p m n", p=P))
+            for m in range(m0, m1):
+                pull_sb[(c, m)] = t[:, m - m0, :]
 
         up_sb = {}
 
@@ -109,7 +131,7 @@ def tile_matting_clipped_step_s3_kernel(
 
         load_act(0, 0, 1)
         load_act(0, 1, 2)
-        load_scales(known_plane, known_scales)
+        load_scales(known_plane[0], known_scales[:, :, :2 * N])
         load_known(0, 1, 0, 2)
         load_act(1, 0, 2)
         load_known(1, 2, 0, 2)
@@ -121,16 +143,19 @@ def tile_matting_clipped_step_s3_kernel(
         load_act(4, 0, 2)
         load_step(1, 0)
         load_step(1, 1)
-        load_pull(0)
-        load_cap()
         load_step(1, 2)
-        load_known(0, 2, 2, 3)
+        load_pull(0)
         load_step(2, 0)
+        load_scales(known_plane[1], known_scales[:, :, 2 * N:])
+        load_known(0, 2, 2, 3)
         load_step(2, 1)
+        load_pull(1, 0, 2)
         load_step(2, 2)
-        load_pull(1)
+        load_pull(1, 2, 4)
+        load_cap()
+        load_pull(2, 0, 2)
         load_up(0)
-        load_pull(2)
+        load_pull(2, 2, 4)
         load_up(1)
 
 
@@ -174,7 +199,8 @@ def tile_matting_clipped_step_s3_kernel(
             step_t[(c, g)] = flow.tile([P, N * PACK], BF16, name="step_t%d_%d" % (c, g), tag="grouped", align_bytes=64)
             d = step_t[(c, g)][:].rearrange("p (a i t) -> p a t i", i=4, t=PACK)
             s = step_raw[(c, g)][:].rearrange("p t (a i) -> p a t i", i=4)
-            nc.scalar.copy(out=d[:, v_cols // 4:], in_=s[:, v_cols // 4:])
+            if v_cols < N:
+                nc.scalar.copy(out=d[:, v_cols // 4:], in_=s[:, v_cols // 4:])
             if v_cols:
                 nc.vector.tensor_copy(out=d[:, :v_cols // 4], in_=s[:, :v_cols // 4])
 
@@ -185,15 +211,17 @@ def tile_matting_clipped_step_s3_kernel(
                 out=step_codes[(c, g)][:].bitcast(FP8X4), scales=step_scales[(c, g)][:], in_=step_t[(c, g)][:]
             )
 
-        z_bank = {}
+        z_bank, z_done = {}, {}
 
-        def z_pass(j, c, ms, first_bank=None):
+        def z_pass(j, c, ms, unused=None):
             for m in ms:
-                if j == 0:
-                    z_bank[(c, m)] = bank(first_bank + m, "z%d_%d" % (c, m))
+                if (c, m) not in z_bank:
+                    z_bank[(c, m)] = bank(4 * (c % 2) + m, "z%d_%d" % (c, m))
+                done = z_done.get((c, m), 0)
+                z_done[(c, m)] = done + 1
                 if j < HG:
                     rhs = known_sb[(j, c)].bitcast(FP4X4)
-                    rhs_scale = known_plane[:, j, c * N:(c + 1) * N]
+                    rhs_scale = known_plane[c // 2][:, j, (c % 2) * N:(c % 2 + 1) * N]
                 else:
                     rhs = step_codes[(c, j - HG)][:].bitcast(FP8X4)
                     rhs_scale = step_scales[(c, j - HG)][:]
@@ -203,8 +231,8 @@ def tile_matting_clipped_step_s3_kernel(
                     lhsT_scale=act_scales[j][:, m * P:(m + 1) * P],
                     rhs=rhs,
                     rhs_scale=rhs_scale,
-                    start=(j == 0),
-                    stop=(j == HG + UG - 1),
+                    start=(done == 0),
+                    stop=(done == HG + UG - 1),
                 )
 
         summed = {}
@@ -214,7 +242,7 @@ def tile_matting_clipped_step_s3_kernel(
             nc.vector.tensor_tensor(
                 out=summed[(c, m)][:].rearrange("r (u p e) -> r u p e", u=2, e=2),
                 in0=z_bank[(c, m)][:].rearrange("r (p u e) -> r u p e", u=2, e=2),
-                in1=pull_sb[c][:, m, :].rearrange("r (p u e) -> r u p e", u=2, e=2),
+                in1=pull_sb[(c, m)].rearrange("r (p u e) -> r u p e", u=2, e=2),
                 op=ALU.add,
             )
 
@@ -312,62 +340,65 @@ def tile_matting_clipped_step_s3_kernel(
             out_act(j, 0, "S")
             out_act(j, 1, e1)
 
+        warm(4, 0)
         act(0, "S")
+        warm(5, 1)
         quant_act(0, 0, 1)
         quant_act(0, 1, 2)
-        z_pass(0, 0, [0, 1], 0)
-        z_pass(0, 1, [0], 4)
+        z_pass(0, 0, [0, 1])
+        z_pass(0, 1, [0])
         act(1, "V")
-        z_pass(0, 1, [1], 4)
-        z_pass(0, 0, [2, 3], 0)
+        z_pass(0, 1, [1])
+        z_pass(0, 0, [2, 3])
         weave(0, 0, 256)
         quant_act(1)
         act(2, "S")
         quant_step(0, 0)
         z_pass(1, 0, ALL)
         z_pass(1, 1, [0, 1])
-        weave(0, 1, 352)
+        weave(0, 1, 256)
         quant_act(2)
+        weave(0, 2, 384)
         act(3, "S")
         quant_step(0, 1)
         z_pass(2, 0, ALL)
-        weave(0, 2, 352)
+        quant_step(0, 2)
         quant_act(3)
         act(4, "S")
-        quant_step(0, 2)
         z_pass(3, 0, ALL)
-        weave(1, 0, 352)
+        weave(1, 0, 384)
         quant_act(4)
-        z_pass(0, 1, [2, 3], 4)
+        z_pass(0, 1, [2, 3])
         z_pass(1, 1, [2, 3])
+        weave(1, 1, 256)
         quant_step(1, 0)
         z_pass(4, 0, ALL)
-        weave(1, 1, 256)
         z_pass(2, 1, ALL)
-        weave(1, 2, 192)
+        weave(1, 2, 256)
         quant_step(1, 1)
         add_pull(0, 0)
         z_pass(3, 1, ALL)
         quant_step(1, 2)
-        add_pull(0, 1)
         z_pass(4, 1, ALL)
-        weave(2, 0, 128)
+        weave(2, 0, 0)
+        add_pull(0, 1)
         add_pull(0, 2)
         add_pull(0, 3)
-        z_pass(0, 2, ALL, 0)
+        z_pass(0, 2, ALL)
         z_pass(1, 2, ALL)
         quant_step(2, 0)
-        weave(2, 1, 64)
+        weave(2, 1, 128)
         add_pull(1, 0)
-        quant_step(2, 1)
-        weave(2, 2, 64)
         add_pull(1, 1)
-        z_pass(2, 2, ALL)
+        quant_step(2, 1)
+        weave(2, 2, 128)
+        z_pass(2, 2, [0, 1])
         low = [((0, m), (1, m)) for m in ALL]
         top = [((2, m),) for m in ALL]
         pair = ((2, 2), (2, 3))
         turn_new(low[0], 4)
         turn_new(low[1], 5)
+        z_pass(2, 2, [2, 3])
         out_new(low[0])
         out_new(low[1])
         add_pull(1, 2)
@@ -377,48 +408,51 @@ def tile_matting_clipped_step_s3_kernel(
         z_pass(4, 2, [0])
         z_pass(3, 2, [3])
         z_pass(4, 2, [1, 2, 3])
-        add_pull(2, 0)
         clip_new(low[0])
-        quant_new(low[0])
+        add_pull(2, 0)
         add_pull(2, 1)
+        quant_new(low[0])
         turn_new(low[2], 6)
         turn_new(low[3], 7)
         turn_new(top[0], 0)
+        turn_new(top[1], 1)
         out_new(top[0])
+        out_new(top[1])
         out_new(low[2])
+        clip_new(low[1])
+        add_pull(2, 2)
+        quant_new(low[1])
+        clip_new(top[0])
         up_pass(0, 0, [0, 1], 4)
         up_pass(0, 1, [0, 1], 5)
-        turn_new(top[1], 1)
-        out_new(top[1])
-        out_new(low[3])
-        clip_new(low[1])
-        clip_new(top[0])
-        quant_new(low[1])
-        quant_new(top[0])
-        up_pass(0, 2, [0, 1], 0)
-        up_pass(0, 0, [2])
-        up_pass(0, 1, [2])
-        up_pass(0, 2, [2])
-        add_pull(2, 2)
+        up_pass(1, 0, [0, 1], 0)
+        up_pass(1, 1, [0, 1], 1)
         clip_new(top[1])
+        quant_new(top[0])
         add_pull(2, 3)
         quant_new(top[1])
-        store(0, 0, "S")
-        store(0, 1, "S")
-        up_pass(0, 3, range(UG), 1)
-        turn_new(pair, 2)
-        out_new(pair)
         clip_new(low[2])
-        store(0, 2, "V")
+        up_pass(0, 0, [2])
+        up_pass(0, 1, [2])
+        up_pass(1, 0, [2])
+        up_pass(1, 1, [2])
+        turn_new(pair, 2)
+        out_new(low[3])
+        store(0, 0, "V")
         quant_new(low[2])
-        store(0, 3, "S")
+        store(0, 1, "S")
+        store(1, 0, "V")
+        out_new(pair)
+        store(1, 1, "V")
         clip_new(pair)
-        clip_new(low[3])
-        quant_new(pair)
-        quant_new(low[3])
-        rest = [(m, f) for m in (1, 2, 3) for f in range(FT)]
-        banks = [3, 4, 5, 6, 0, 1, 7, 2]
+        rest = [(0, 2), (0, 3), (1, 2), (1, 3)] + [(m, f) for m in (2, 3) for f in range(FT)]
+        banks = [3, 6, 4, 7, 5, 0, 1, 2]
         for i, (m, f) in enumerate(rest[:-1]):
             up_pass(m, f, range(UG), banks[i % 8])
             store(m, f, "S" if i % 2 == 0 else "V")
-        narrow(3, 3, [6, 0, 1, 7])
+            if i == 1:
+                quant_new(pair)
+                clip_new(low[3])
+            if i == 3:
+                quant_new(low[3])
+        narrow(3, 3, [7, 5, 0, 1])

@@ -46,24 +46,6 @@ def tile_matting_clipped_step_s3_kernel(
         known_plane = [kept("known_plane0", [P, HG, 2 * N], U8), kept("known_plane1", [P, HG, N], U8)]
         up_plane = [kept("up_plane%d" % h, [P, UG, F // 2], U8) for h in range(2)]
         nc.vector.memset(known_plane[0][:].bitcast(I32), 0)
-        warm_in = kept("warm_in", [P, 2 * KP], BF16)
-        warm_codes = kept("warm_codes", [P, 2 * P], U32)
-        warm_scales = kept("warm_scales", [P, 2 * P], U8)
-        nc.vector.memset(warm_in[:], 0.0)
-        nc.vector.quantize_mx(out=warm_codes[:].bitcast(FP8X4), scales=warm_scales[:], in_=warm_in[:])
-
-        def warm(n, b):
-            sink = bank(b, "warm%d" % b)
-            for i in range(n):
-                nc.tensor.matmul_mx(
-                    out=sink[:, :2 * P],
-                    lhsT=warm_codes[:, :P].bitcast(FP8X4),
-                    lhsT_scale=warm_scales[:, :P],
-                    rhs=warm_codes[:].bitcast(FP8X4),
-                    rhs_scale=warm_scales[:],
-                    start=True,
-                    stop=True,
-                )
 
         nc.vector.memset(known_plane[1][:].bitcast(I32), 0)
         for h in range(2):
@@ -134,9 +116,9 @@ def tile_matting_clipped_step_s3_kernel(
         load_scales(known_plane[0], known_scales[:, :, :2 * N])
         load_known(0, 1, 0, 2)
         load_act(1, 0, 2)
-        load_known(1, 2, 0, 2)
         load_step(0, 0)
         load_act(2, 0, 2)
+        load_known(1, 2, 0, 2)
         load_step(0, 1)
         load_act(3, 0, 2)
         load_step(0, 2)
@@ -340,17 +322,18 @@ def tile_matting_clipped_step_s3_kernel(
             out_act(j, 0, "S")
             out_act(j, 1, e1)
 
-        warm(4, 0)
         act(0, "S")
-        warm(5, 1)
         quant_act(0, 0, 1)
         quant_act(0, 1, 2)
         z_pass(0, 0, [0, 1])
         z_pass(0, 1, [0])
-        act(1, "V")
+        turn_act(1, 0, 6)
+        turn_act(1, 1, 7)
+        out_act(1, 0, "S")
+        weave(0, 0, 192)
+        out_act(1, 1, "V")
         z_pass(0, 1, [1])
         z_pass(0, 0, [2, 3])
-        weave(0, 0, 256)
         quant_act(1)
         act(2, "S")
         quant_step(0, 0)
@@ -358,15 +341,15 @@ def tile_matting_clipped_step_s3_kernel(
         z_pass(1, 1, [0, 1])
         weave(0, 1, 256)
         quant_act(2)
-        weave(0, 2, 384)
         act(3, "S")
         quant_step(0, 1)
+        weave(0, 2, 384)
         z_pass(2, 0, ALL)
-        quant_step(0, 2)
         quant_act(3)
+        quant_step(0, 2)
         act(4, "S")
         z_pass(3, 0, ALL)
-        weave(1, 0, 384)
+        weave(1, 0, 320)
         quant_act(4)
         z_pass(0, 1, [2, 3])
         z_pass(1, 1, [2, 3])

from contextlib import ExitStack

import concourse.mybir as mybir
from concourse.masks import make_identity

M, U, H, F = 512, 1536, 1024, 2048
FLOPS = 2 * M * (U * U + H * U + U * F)

F32 = mybir.dt.float32
BF16 = mybir.dt.bfloat16
I32 = mybir.dt.int32
U32 = mybir.dt.uint32
U8 = mybir.dt.uint8
FP8X4 = mybir.dt.float8_e4m3fn_x4
FP4X4 = mybir.dt.float4_e2m1fn_x4
ALU = mybir.AluOpType

P = 128
PACK = 4
KP = P * PACK
N = 512
MT = M // P
HG = H // KP
UG = U // KP
FT = F // N


def tile_matting_clipped_step_s3_kernel(
    tc, alpha, fixed, step, known_words, known_scales, pull, cap, up_words, up_scales, out
):
    nc = tc.nc
    with ExitStack() as ctx:
        keep = ctx.enter_context(tc.tile_pool(name="keep", bufs=1))
        flow = ctx.enter_context(tc.tile_pool(name="flow", bufs=4))
        psum = ctx.enter_context(tc.psum_pool(name="psum", bufs=1))
        ctx.enter_context(tc.manual_schedule())

        def kept(name, shape, dtype):
            return keep.tile(shape, dtype, name=name, align_bytes=64)

        def bank(b, name):
            return psum.tile([P, N], F32, name=name, tag="bank%d" % b)

        ident = kept("ident", [P, P], F32)
        make_identity(nc, ident[:])
        known_plane = [kept("known_plane0", [P, HG, 2 * N], U8), kept("known_plane1", [P, HG, N], U8)]
        up_plane = [kept("up_plane%d" % h, [P, UG, F // 2], U8) for h in range(2)]
        nc.vector.memset(known_plane[0][:].bitcast(I32), 0)

        nc.vector.memset(known_plane[1][:].bitcast(I32), 0)
        for h in range(2):
            nc.vector.memset(up_plane[h][:].bitcast(I32), 0)

        act_raw = {}

        def load_act(j, h0, h1):
            src = fixed[:, j * KP:(j + 1) * KP] if j < HG else alpha[:, (j - HG) * KP:(j - HG + 1) * KP]
            t = kept("act_raw%d_%d" % (j, h0), [P, 2 * (h1 - h0), KP], BF16)
            nc.sync.dma_start(out=t[:], in_=src.rearrange("(m p) k -> p m k", p=P)[:, 2 * h0:2 * h1, :])
            for h in range(h0, h1):
                act_raw[(j, h)] = t[:, 2 * (h - h0):2 * (h - h0) + 2, :]

        def load_scales(plane, scales):
            for q in range(4):
                nc.sync.dma_start(
                    out=plane[32 * q:32 * q + 4].bitcast(I32),
                    in_=scales[:, 4 * q:4 * q + 4, :].rearrange("g r n -> r g n").bitcast(I32),
                )

        known_sb = {}

        def load_known(g0, g1, c0, c1):
            t = kept("known%d_%d" % (g0, c0), [P, g1 - g0, 2 * N * (c1 - c0)], U8)
            nc.sync.dma_start(
                out=t[:].bitcast(I32),
                in_=known_words[g0:g1, :, 2 * N * c0:2 * N * c1].rearrange("g p n -> p g n").bitcast(I32),
            )
            for g in range(g0, g1):
                for c in range(c0, c1):
                    known_sb[(g, c)] = t[:, g - g0, 2 * N * (c - c0):2 * N * (c - c0 + 1)]

        step_raw = {}

        def load_step(c, g):
            step_raw[(c, g)] = kept("step_raw%d_%d" % (c, g), [P, PACK, N], BF16)
            rows = step[g * KP:(g + 1) * KP, c * N:(c + 1) * N]
            nc.sync.dma_start(out=step_raw[(c, g)][:], in_=rows.rearrange("(p t) n -> p t n", t=PACK))

        pull_sb = {}

        def load_pull(c, m0=0, m1=MT):
            t = kept("pull%d_%d" % (c, m0), [P, m1 - m0, N], BF16)
            rows = pull[m0 * P:m1 * P, c * N:(c + 1) * N]
            nc.sync.dma_start(out=t[:], in_=rows.rearrange("(m p) n -> p m n", p=P))
            for m in range(m0, m1):
                pull_sb[(c, m)] = t[:, m - m0, :]

        up_sb = {}

        def load_up(h):
            load_scales(up_plane[h], up_scales[:, :, h * (F // 2):(h + 1) * (F // 2)])
            up_sb[h] = kept("up%d" % h, [P, UG, F], U8)
            nc.sync.dma_start(
                out=up_sb[h][:].bitcast(I32),
                in_=up_words[:, :, h * F:(h + 1) * F].rearrange("g p n -> p g n").bitcast(I32),
            )

        cap_sb = kept("cap_sb", [P, UG, PACK], BF16)

        def load_cap():
            nc.sync.dma_start(out=cap_sb[:], in_=cap.rearrange("(g p t) -> p g t", p=P, t=PACK))


        load_act(0, 0, 1)
        load_act(0, 1, 2)
        load_scales(known_plane[0], known_scales[:, :, :2 * N])
        load_known(0, 1, 0, 2)
        load_act(1, 0, 2)
        load_step(0, 0)
        load_act(2, 0, 2)
        load_known(1, 2, 0, 2)
        load_step(0, 1)
        load_act(3, 0, 2)
        load_step(0, 2)
        load_act(4, 0, 2)
        load_step(1, 0)
        load_step(1, 1)
        load_step(1, 2)
        load_pull(0)
        load_step(2, 0)
        load_scales(known_plane[1], known_scales[:, :, 2 * N:])
        load_known(0, 2, 2, 3)
        load_step(2, 1)
        load_pull(1, 0, 2)
        load_step(2, 2)
        load_pull(1, 2, 4)
        load_cap()
        load_pull(2, 0, 2)
        load_up(0)
        load_pull(2, 2, 4)
        load_up(1)


        def words_out(engine, dst, src_bank, n_ops):
            d = dst.bitcast(F32).rearrange("p (o r u) -> p o r u", o=n_ops, u=2)
            s = src_bank[:, :n_ops * 2 * P].rearrange("p (o u r) -> p o r u", o=n_ops, u=2)
            if engine == "S":
                nc.scalar.copy(out=d, in_=s)
            else:
                nc.vector.tensor_copy(out=d, in_=s)

        act_t, act_codes, act_scales, act_bank = {}, {}, {}, {}

        def turn_act(j, h, b):
            act_bank[(j, h)] = bank(b, "act_bank%d_%d" % (j, h))
            for o in range(2):
                words = act_raw[(j, h)][:, o, :].bitcast(F32)
                for u in range(2):
                    s = 2 * o + u
                    nc.tensor.transpose(act_bank[(j, h)][:, s * P:(s + 1) * P], words[:, u::2], ident[:])

        def out_act(j, h, engine):
            if h == 0:
                act_t[j] = flow.tile([P, MT * KP], BF16, name="act_t%d" % j, tag="grouped", align_bytes=64)
            words_out(engine, act_t[j][:, 2 * h * KP:2 * (h + 1) * KP], act_bank[(j, h)], 2)

        def quant_act(j, h0=0, h1=2):
            if h0 == 0:
                act_codes[j] = kept("act_codes%d" % j, [P, M], U32)
                act_scales[j] = kept("act_scales%d" % j, [P, M], U8)
            cols = slice(2 * h0 * P, 2 * h1 * P)
            nc.vector.quantize_mx(
                out=act_codes[j][:, cols].bitcast(FP8X4),
                scales=act_scales[j][:, cols],
                in_=act_t[j][:, 2 * h0 * KP:2 * h1 * KP],
            )

        step_t, step_codes, step_scales = {}, {}, {}

        def weave(c, g, v_cols):
            step_t[(c, g)] = flow.tile([P, N * PACK], BF16, name="step_t%d_%d" % (c, g), tag="grouped", align_bytes=64)
            d = step_t[(c, g)][:].rearrange("p (a i t) -> p a t i", i=4, t=PACK)
            s = step_raw[(c, g)][:].rearrange("p t (a i) -> p a t i", i=4)
            if v_cols < N:
                nc.scalar.copy(out=d[:, v_cols // 4:], in_=s[:, v_cols // 4:])
            if v_cols:
                nc.vector.tensor_copy(out=d[:, :v_cols // 4], in_=s[:, :v_cols // 4])

        def quant_step(c, g):
            step_codes[(c, g)] = kept("step_codes%d_%d" % (c, g), [P, N], U32)
            step_scales[(c, g)] = kept("step_scales%d_%d" % (c, g), [P, N], U8)
            nc.vector.quantize_mx(
                out=step_codes[(c, g)][:].bitcast(FP8X4), scales=step_scales[(c, g)][:], in_=step_t[(c, g)][:]
            )

        z_bank, z_done = {}, {}

        def z_pass(j, c, ms, unused=None):
            for m in ms:
                if (c, m) not in z_bank:
                    z_bank[(c, m)] = bank(4 * (c % 2) + m, "z%d_%d" % (c, m))
                done = z_done.get((c, m), 0)
                z_done[(c, m)] = done + 1
                if j < HG:
                    rhs = known_sb[(j, c)].bitcast(FP4X4)
                    rhs_scale = known_plane[c // 2][:, j, (c % 2) * N:(c % 2 + 1) * N]
                else:
                    rhs = step_codes[(c, j - HG)][:].bitcast(FP8X4)
                    rhs_scale = step_scales[(c, j - HG)][:]
                nc.tensor.matmul_mx(
                    out=z_bank[(c, m)][:],
                    lhsT=act_codes[j][:, m * P:(m + 1) * P].bitcast(FP8X4),
                    lhsT_scale=act_scales[j][:, m * P:(m + 1) * P],
                    rhs=rhs,
                    rhs_scale=rhs_scale,
                    start=(done == 0),
                    stop=(done == HG + UG - 1),
                )

        summed = {}

        def add_pull(c, m):
            summed[(c, m)] = kept("summed%d_%d" % (c, m), [P, N], BF16)
            nc.vector.tensor_tensor(
                out=summed[(c, m)][:].rearrange("r (u p e) -> r u p e", u=2, e=2),
                in0=z_bank[(c, m)][:].rearrange("r (p u e) -> r u p e", u=2, e=2),
                in1=pull_sb[(c, m)].rearrange("r (p u e) -> r u p e", u=2, e=2),
                op=ALU.add,
            )

        new_bank, new_t, new_clip, new_codes, new_scales = {}, {}, {}, {}, {}

        def turn_new(ops, b):
            new_bank[ops] = bank(b, "new_bank%d_%d" % ops[0])
            for o, cm in enumerate(ops):
                words = summed[cm][:].bitcast(F32)
                for u in range(2):
                    s = 2 * o + u
                    nc.tensor.transpose(new_bank[ops][:, s * P:(s + 1) * P], words[:, u * P:(u + 1) * P], ident[:])

        def out_new(ops):
            new_t[ops] = kept("new_t%d_%d" % ops[0], [P, len(ops) * KP], BF16)
            pairs = new_bank[ops][:].bitcast(BF16)
            for o in range(len(ops)):
                nc.scalar.activation(
                    out=new_t[ops][:, o * KP:(o + 1) * KP].rearrange("p (r u e) -> p r u e", u=2, e=2),
                    in_=pairs[:, o * KP:(o + 1) * KP].rearrange("p (u r e) -> p r u e", u=2, e=2),
                    func=mybir.ActivationFunctionType.Relu,
                )

        def clip_new(ops):
            new_clip[ops] = kept("new_clip%d_%d" % ops[0], [P, len(ops) * KP], BF16)
            c0 = ops[0][0]
            c1 = ops[-1][0] + 1
            caps = cap_sb[:, c0:c1, :].unsqueeze(2).to_broadcast([P, len(ops), P, PACK])
            nc.vector.tensor_tensor(
                out=new_clip[ops][:].rearrange("p (o r t) -> p o r t", r=P, t=PACK),
                in0=new_t[ops][:].rearrange("p (o r t) -> p o r t", r=P, t=PACK),
                in1=caps,
                op=ALU.min,
            )

        def quant_new(ops):
            codes = kept("new_codes%d_%d" % ops[0], [P, len(ops) * P], U32)
            scales = kept("new_scales%d_%d" % ops[0], [P, len(ops) * P], U8)
            nc.vector.quantize_mx(out=codes[:].bitcast(FP8X4), scales=scales[:], in_=new_clip[ops][:])
            for o, cm in enumerate(ops):
                new_codes[cm] = codes[:, o * P:(o + 1) * P]
                new_scales[cm] = scales[:, o * P:(o + 1) * P]

        out_bank = {}

        def up_pass(m, f, gs, b=None):
            h, fh = divmod(f, 2)
            for g in gs:
                if g == 0:
                    out_bank[(m, f)] = bank(b, "out%d_%d" % (m, f))
                nc.tensor.matmul_mx(
                    out=out_bank[(m, f)][:],
                    lhsT=new_codes[(g, m)].bitcast(FP8X4),
                    lhsT_scale=new_scales[(g, m)],
                    rhs=up_sb[h][:, g, 2 * fh * N:2 * (fh + 1) * N].bitcast(FP4X4),
                    rhs_scale=up_plane[h][:, g, fh * N:(fh + 1) * N],
                    start=(g == 0),
                    stop=(g == UG - 1),
                )

        def leave(src, m, col, width, engine):
            res = flow.tile([P, width], F32, name="res%d_%d" % (m, col), tag="res", bufs=16)
            if engine == "S":
                nc.scalar.copy(out=res[:], in_=src)
            else:
                nc.vector.tensor_copy(out=res[:], in_=src)
            nc.sync.dma_start(out=out[m * P:(m + 1) * P, col:col + width], in_=res[:])

        def store(m, f, engine):
            leave(out_bank[(m, f)][:], m, f * N, N, engine)

        def narrow(m, f, banks):
            h, fh = divmod(f, 2)
            for i, b in enumerate(banks):
                acc = bank(b, "tail%d" % i)
                col = fh * N + i * P
                for g in range(UG):
                    nc.tensor.matmul_mx(
                        out=acc[:, :P],
                        lhsT=new_codes[(g, m)].bitcast(FP8X4),
                        lhsT_scale=new_scales[(g, m)],
                        rhs=up_sb[h][:, g, 2 * col:2 * (col + P)].bitcast(FP4X4),
                        rhs_scale=up_plane[h][:, g, col:col + P],
                        start=(g == 0),
                        stop=(g == UG - 1),
                    )
                leave(acc[:, :P], m, f * N + i * P, P, "V" if i % 2 == 0 else "S")


        ALL = range(MT)

        def act(j, e1):
            turn_act(j, 0, 6)
            turn_act(j, 1, 7)
            out_act(j, 0, "S")
            out_act(j, 1, e1)

        act(0, "S")
        quant_act(0, 0, 1)
        quant_act(0, 1, 2)
        z_pass(0, 0, [0, 1])
        z_pass(0, 1, [0])
        turn_act(1, 0, 6)
        turn_act(1, 1, 7)
        out_act(1, 0, "S")
        weave(0, 0, 192)
        out_act(1, 1, "V")
        z_pass(0, 1, [1])
        z_pass(0, 0, [2, 3])
        quant_act(1)
        act(2, "S")
        quant_step(0, 0)
        z_pass(1, 0, ALL)
        z_pass(1, 1, [0, 1])
        weave(0, 1, 256)
        quant_act(2)
        act(3, "S")
        quant_step(0, 1)
        weave(0, 2, 384)
        z_pass(2, 0, ALL)
        quant_act(3)
        quant_step(0, 2)
        act(4, "S")
        z_pass(3, 0, ALL)
        weave(1, 0, 320)
        quant_act(4)
        z_pass(0, 1, [2, 3])
        z_pass(1, 1, [2, 3])
        weave(1, 1, 256)
        quant_step(1, 0)
        z_pass(4, 0, ALL)
        z_pass(2, 1, ALL)
        weave(1, 2, 256)
        quant_step(1, 1)
        add_pull(0, 0)
        z_pass(3, 1, ALL)
        quant_step(1, 2)
        z_pass(4, 1, ALL)
        weave(2, 0, 0)
        add_pull(0, 1)
        add_pull(0, 2)
        add_pull(0, 3)
        z_pass(0, 2, ALL)
        z_pass(1, 2, ALL)
        quant_step(2, 0)
        weave(2, 1, 128)
        add_pull(1, 0)
        add_pull(1, 1)
        quant_step(2, 1)
        weave(2, 2, 128)
        z_pass(2, 2, [0, 1])
        low = [((0, m), (1, m)) for m in ALL]
        top = [((2, m),) for m in ALL]
        pair = ((2, 2), (2, 3))
        turn_new(low[0], 4)
        turn_new(low[1], 5)
        z_pass(2, 2, [2, 3])
        out_new(low[0])
        out_new(low[1])
        add_pull(1, 2)
        quant_step(2, 2)
        add_pull(1, 3)
        z_pass(3, 2, [0, 1, 2])
        z_pass(4, 2, [0])
        z_pass(3, 2, [3])
        z_pass(4, 2, [1, 2, 3])
        clip_new(low[0])
        add_pull(2, 0)
        add_pull(2, 1)
        quant_new(low[0])
        turn_new(low[2], 6)
        turn_new(low[3], 7)
        turn_new(top[0], 0)
        turn_new(top[1], 1)
        out_new(top[0])
        out_new(top[1])
        out_new(low[2])
        clip_new(low[1])
        add_pull(2, 2)
        quant_new(low[1])
        clip_new(top[0])
        up_pass(0, 0, [0, 1], 4)
        up_pass(0, 1, [0, 1], 5)
        up_pass(1, 0, [0, 1], 0)
        up_pass(1, 1, [0, 1], 1)
        clip_new(top[1])
        quant_new(top[0])
        add_pull(2, 3)
        quant_new(top[1])
        clip_new(low[2])
        up_pass(0, 0, [2])
        up_pass(0, 1, [2])
        up_pass(1, 0, [2])
        up_pass(1, 1, [2])
        turn_new(pair, 2)
        out_new(low[3])
        store(0, 0, "V")
        quant_new(low[2])
        store(0, 1, "S")
        store(1, 0, "V")
        out_new(pair)
        store(1, 1, "V")
        clip_new(pair)
        rest = [(0, 2), (0, 3), (1, 2), (1, 3)] + [(m, f) for m in (2, 3) for f in range(FT)]
        banks = [3, 6, 4, 7, 5, 0, 1, 2]
        for i, (m, f) in enumerate(rest[:-1]):
            up_pass(m, f, range(UG), banks[i % 8])
            store(m, f, "S" if i % 2 == 0 else "V")
            if i == 1:
                quant_new(pair)
                clip_new(low[3])
            if i == 3:
                quant_new(low[3])
        narrow(3, 3, [7, 5, 0, 1])
